import numpy as np, ml_dtypes
CORES = [8,9,10,11,12,13]
N = 6
BF = ml_dtypes.bfloat16
W, C, RU, S, M = 8192, 256, 2, 3, 3
def bf(x):
    return np.ascontiguousarray(x).astype(np.float32).astype(BF)
def parts(rng):
    d = {"ends": rng.integers(0, 256, (N, 8, 16, C)), "db": rng.integers(0, 256, (N, 8, 16, W), dtype=np.int16)}
    d["db"][:, :, 15] = rng.integers(0, M + 1, (N, 8, W)) * (rng.random((N, 8, W)) < 0.75)
    d["wt"] = rng.integers(0, rng.choice(np.array([2, 6, 12, 18]), (N, 8, 1, 16)), (N, 8, 16, 16))
    d["salt"] = rng.integers(0, W, (N, 8, 16, C)); d["nz"] = rng.integers(0, 256, (N, 8, 16, RU, S, C))
    k = rng.random((N, 8, RU, C))
    d["sl"] = np.where(k < 0.0625, 4000, np.where(k > 0.9375, -4000, rng.integers(-700, 401, (N, 8, RU, C))))
    return d
def pack(d):
    for k in ("ends", "wt", "nz"): d[k][:, :, 15] = 0
    return {"ends": bf(d["ends"].reshape(N, 128, C)), "db": bf(d["db"].reshape(N, 128, W)), "wt": bf(d["wt"].reshape(N, 128, 16)),
            "salt": np.ascontiguousarray(d["salt"].reshape(N, 128, C)).astype(np.int32), "nz": bf(d["nz"].reshape(N, 128, RU * S * C)),
            "sl": np.ascontiguousarray(d["sl"].reshape(N, 8, RU * C)).astype(np.int32)}
def walk(e, D, wt, salt, nz, sl, delta=None):
    e = e.astype(np.int32); D = D.astype(np.int32); w = wt.astype(np.int32).transpose(0, 1, 3, 2); a = salt.astype(np.int32); z = nz.astype(np.int32)
    verdicts, places = [], []
    for m in range(RU):
        v = np.roll(e, 1, axis=0); t = np.roll(e, -1, axis=0)
        shadow = []
        for s in range(S):
            u = np.matmul(w, v) >> 6
            pl = ((u * u >> 3) + 37 * u + 211 * s + a) & (W - 1)
            got = np.take_along_axis(D, pl.transpose(0, 1, 3, 2).reshape(N, 8, 1, C * 16), 3).reshape(N, 8, 16, C, 16)
            ask = (u & M).transpose(0, 1, 3, 2)
            hit = (got[:, :, 15] == ask) & (((np.arange(C) + m) & 3) != s)[:, None]
            f = (v + z[:, :, :, m, s]) & 255
            x = np.where(hit[:, :, None], got, f[..., None])
            first = np.argmin(hit, axis=3)
            place = np.take_along_axis(pl, first[:, :, None, :], 2)[:, :, 0]
            rec = f + 0; rec[:, :, 15] = np.take_along_axis(ask, first[..., None], 3)[..., 0]
            place = np.where(np.all(hit, axis=3), -1, place)
            shadow.append((place, rec)); places.append(place)
            v = (2 * v + np.max(x, axis=4) + np.min(x, axis=4)) >> 2; v[:, :, 15] = 0
        A = np.sum(np.abs(v - t), axis=2); B = np.sum(np.abs(e - t), axis=2)
        if delta is not None: sl[:, :, m] = A - B + delta[:, :, m]
        ok = A <= B + sl[:, :, m]
        e = np.where(ok[:, :, None], v, e); verdicts.append(ok)
        for place, rec in shadow:
            for q in range(N):
                for g in range(8):
                    c = np.flatnonzero(ok[q, g] & (place[q, g] >= 0))
                    to, at = np.unique(place[q, g, c], return_index=True)
                    D[q, g][:, to] = rec[q, g][:, c[at]]
    return e, np.stack(verdicts, 2), np.stack(places, 2)
def setup_inputs(rng):
    return pack(parts(rng))
def setup_inputs_again(rng):
    d = parts(rng)
    turn = (np.arange(N)[:, None, None, None] + np.arange(8)[:, None, None] + np.arange(RU)[:, None]) & 1
    d["sl"] = np.where(rng.random((N, 8, RU, C)) < 0.875, np.where(turn == 1, 4000, -4000), d["sl"])
    return pack(d)
def setup_inputs_alike(rng):
    d = parts(rng); c = np.arange(C)
    d["wt"][:, :3] = 0
    d["salt"][:, :3] = (rng.integers(0, W, (N, 3, 16, 1)) + 211 * (c & 3) * (np.arange(3)[:, None, None] > 0)) & (W - 1)
    d["db"][::2, 0, 15] = rng.integers(1, M + 1, d["db"][::2, 0, 15].shape); d["sl"][::2, 0, 0] = 4000
    ix = rng.integers(0, 4, C)
    d["ends"][:, 3:6] = d["ends"][:, 3:6][..., ix]; d["salt"][:, 3:6] = d["salt"][:, 3:6][..., ix]
    d["wt"][:, 6] = d["wt"][:, 6][:, :, :1] + np.zeros((1, 1, 16), np.int64); d["salt"][:, 6] = d["salt"][:, 6][:, :1] + np.zeros((1, 16, 1), np.int64)
    d["wt"][:, 7] = 0; d["db"][:, 7, 15] = rng.integers(1, M + 1, (N, W))
    x = 8 * np.argsort(rng.random((N, W // 8)), axis=1)[:, :C]
    for p in range(4):
        d["salt"][:, 7, p] = (x - 211 * p) & (W - 1)
        for q in range(N):
            if p > 0: d["db"][q, 7, 15, (x[q] + 211 * p) & (W - 1)] = 0
    d["sl"][:, 7] = np.where(rng.random((N, RU, C)) < 0.75, 4000, d["sl"][:, 7])
    return pack(d)
def setup_inputs_full(rng):
    d = parts(rng); c = np.arange(C)
    d["wt"][:, 0] = 0; d["db"][:, 0, 15] = 0
    d["wt"][:, 1] = 0; d["db"][:, 1, 15] = rng.integers(1, M + 1, (N, W))
    d["wt"][:, 2] = 0; d["wt"][:, 2, :, 15] = rng.integers(1, 18, (N, 16)); d["db"][:, 2, 15] = 0
    d["wt"][:, 3] = 17; d["ends"][:, 3, :, c % 2 == 0] = 255; d["nz"][:, 3, :, :, :, c % 2 == 0] = 0
    d["db"][:, 3, :15] = 255 - rng.integers(0, 5, (N, 15, W)) * (np.arange(N) & 1)[:, None, None]
    d["db"][:, 4, :15] = 255 * rng.integers(0, 2, (N, 15, W)); d["ends"][:, 4] = 255 * rng.integers(0, 2, (N, 16, C))
    d["ends"][:, 5, :, c % 2 == 0] = 0; d["nz"][:, 5, :, :, :, c % 2 == 0] = 0
    d["salt"][:, :2] = np.where(rng.random((N, 2, 16, C)) < 0.5, (W - 1) * rng.integers(0, 2, (N, 2, 16, C)), d["salt"][:, :2])
    d["salt"][:, 0, 0] = (W - 1) * (((c >> 2) + np.arange(N)[:, None]) & 1)
    d["wt"][:, 6] = 0; d["db"][:, 6, 15] = rng.integers(1, M + 1, (N, W))
    d["salt"][:, 6, 0] = 8 * np.argsort(rng.random((N, W // 8)), axis=1)[:, :C] + rng.integers(0, 8, (N, 1))
    d["sl"][:, 6, 0] = np.where((np.arange(N) & 1) == 0, 4000, -4000)[:, None]
    return pack(d)
def setup_inputs_ties(rng):
    d = parts(rng); r = np.arange(N)
    d["ends"][:, 0] = 0; d["nz"][:, 0] = 0; d["db"][:, 0, :15] = 0
    for g, b in ((1, (r >> 1) & 1), (2, r & 1)):
        b = b[:, None, None]
        d["ends"][:, g] = np.abs(255 * b - rng.integers(0, 16, (N, 16, C))); d["nz"][:, g] = 0
        d["db"][:, g, :15] = np.abs(255 * np.roll(b, 1, axis=0) - rng.integers(0, 16, (N, 15, W)))
    for k in ("ends", "wt", "nz"): d[k][:, :, 15] = 0
    walk(d["ends"], d["db"], d["wt"], d["salt"], d["nz"], d["sl"], rng.integers(-1, 2, (N, 8, RU, C)))
    return pack(d)
def setup_inputs_spread(rng):
    d = parts(rng)
    d["ends"] = (np.exp2(8 * rng.random((N, 8, 1, C))) * rng.random((N, 8, 16, C))).astype(np.int64)
    d["nz"] = (np.exp2(8 * rng.random((N, 8, 1, RU, S, C))) * rng.random((N, 8, 16, RU, S, C))).astype(np.int64)
    d["db"] = (np.exp2(8 * rng.random((N, 8, 1, W))) * rng.random((N, 8, 16, W))).astype(np.int16)
    d["db"][:, :, 15] = np.minimum((M + 1) * rng.random((N, 8, W)) ** rng.choice(np.array([0.5, 1.0, 3.0]), (N, 8, 1)), M).astype(np.int16)
    d["wt"] = np.minimum((np.exp2(4.2 * rng.random((N, 8, 1, 16))) * rng.random((N, 8, 16, 16))).astype(np.int64), 17)
    d["sl"] = rng.integers(-4000, 4001, (N, 8, RU, C))
    return pack(d)
def check_inputs(d):
    bad = []
    for k, lo, hi in (("ends", 0, 255), ("db", 0, 255), ("wt", 0, 17), ("salt", 0, W - 1), ("nz", 0, 255), ("sl", -4000, 4000)):
        x = np.asarray(d[k]).astype(np.float64)
        if not (np.min(x) >= lo and np.max(x) <= hi): bad.append("range of " + k)
        elif np.any(x != np.floor(x)): bad.append("whole numbers in " + k)
    for k, hi in (("ends", 0), ("wt", 0), ("nz", 0), ("db", M)):
        x = np.asarray(d[k]).astype(np.float64).reshape(N, 8, 16, -1)[:, :, 15]
        if not np.max(x) <= hi: bad.append("rows 16*g + 15 of " + k)
    return bad
def reference(ends, db, wt, salt, nz, sl):
    h = [x.astype(np.float32).astype(np.int32) for x in (ends, db, wt, nz)]
    e, ok, place = walk(h[0].reshape(N, 8, 16, C), h[1].reshape(N, 8, 16, W), h[2].reshape(N, 8, 16, 16), salt.reshape(N, 8, 16, C), h[3].reshape(N, 8, 16, RU, S, C), sl.astype(np.int64).reshape(N, 8, RU, C))
    return {"ye": e.reshape(N, 128, C).astype(np.float32).astype(BF), "yv": ok.reshape(N, 8, RU * C).astype(np.float32), "yp": place.reshape(N, 8, RU * S * C).astype(np.float32)}

from concourse.mybir import AluOpType, ActivationFunctionType

A = AluOpType
F = ActivationFunctionType
W, C, RU, S = 8192, 256, 2, 3
K = 16384.0
MG = 12582912.0
DB0 = 64
FS0 = DB0 + W
NSLOT = 18

SCRATCH = {
    "win": ("sbuf", [128, FS0 + 64 * NSLOT], "bfloat16"),
    "eown": ("sbuf", [128, 256], "bfloat16"), "lft0": ("sbuf", [128, 256], "bfloat16"), "rgt0": ("sbuf", [128, 256], "bfloat16"),
    "enew": ("sbuf", [128, 256], "bfloat16"), "lft1": ("sbuf", [128, 256], "bfloat16"), "rgt1": ("sbuf", [128, 256], "bfloat16"),
    "eout": ("sbuf", [128, 256], "bfloat16"),
    "wts": ("sbuf", [128, 16], "bfloat16"), "slt": ("sbuf", [128, 256], "int32"), "nzs": ("sbuf", [128, 1536], "bfloat16"),
    "sli": ("sbuf", [128, 512], "int32"), "slf": ("sbuf", [128, 512], "float32"), "s8": ("sbuf", [128, 768], "float32"),
    "jm": ("sbuf", [128, 128], "float32"), "gm": ("sbuf", [128, 128], "float32"), "pi": ("sbuf", [128, 4], "int32"),
    "j34": ("sbuf", [128, 34], "float32"), "jd": ("sbuf", [128, 256], "float32"), "jd2": ("sbuf", [128, 256], "float32"),
    "jd3": ("sbuf", [128, 256], "float32"),
    "dum0": ("sbuf", [128, 48], "float32"), "dum": ("sbuf", [128, 48], "float32"),
    "fc": ("sbuf", [128, 64 * NSLOT], "float32"), "col": ("sbuf", [128, 16], "float32"),
    "cb": ("sbuf", [128, 15 * 128], "bfloat16"), "cf": ("sbuf", [128, 3 * 128], "float32"),
    "z15": ("sbuf", [128, 144], "bfloat16"), "yy": ("sbuf", [128, 144], "float32"), "yb": ("sbuf", [128, 34], "float32"),
    "cst": ("sbuf", [128, 448], "bfloat16"), "mall": ("sbuf", [128, 64], "bfloat16"),
    "d0x": ("sbuf", [128, 1024], "bfloat16"), "d0n": ("sbuf", [128, 1024], "bfloat16"), "dw": ("sbuf", [128, 1024], "bfloat16"),
    "uf": ("sbuf", [128, 256], "float32"), "kb": ("sbuf", [128, 256], "bfloat16"), "wi": ("sbuf", [128, 256], "int32"),
    "pl": ("sbuf", [128, 256], "int32"), "of1": ("sbuf", [128, 256], "uint16"), "plf": ("sbuf", [128, 256], "float32"),
    "ask": ("sbuf", [128, 256], "bfloat16"), "hh": ("sbuf", [128, 256], "bfloat16"), "fsk": ("sbuf", [128, 256], "bfloat16"),
    "mis": ("sbuf", [128, 256], "bfloat16"), "t3": ("sbuf", [128, 256], "float32"), "of2": ("sbuf", [128, 256], "uint16"),
    "x1": ("sbuf", [128, 4096], "bfloat16"), "x2": ("sbuf", [128, 4096], "bfloat16"),
    "hi": ("sbuf", [128, 4096], "bfloat16"), "lo": ("sbuf", [128, 4096], "bfloat16"),
    "vb": ("sbuf", [128, 768], "bfloat16"), "mm": ("sbuf", [128, 1536], "float32"), "m2": ("sbuf", [128, 256], "bfloat16"),
    "fsh": ("sbuf", [128, 768], "bfloat16"), "da": ("sbuf", [128, 256], "bfloat16"), "dbb": ("sbuf", [128, 256], "bfloat16"),
    "nac": ("sbuf", [128, 256], "bfloat16"), "td": ("sbuf", [128, 256], "bfloat16"),
    "st0": ("sbuf", [128, 256], "float32"), "st1": ("sbuf", [128, 256], "float32"), "sv": ("sbuf", [128, 512], "float32"),
    "pc": ("sbuf", [128, 48], "float32"), "nb": ("sbuf", [128, 48], "float32"),
    "ab": ("sbuf", [128, 3072], "bfloat16"), "sc": ("sbuf", [128, 3072], "bfloat16"),
    "wn": ("sbuf", [128, 48], "float32"), "wp": ("sbuf", [128, 48], "float32"), "wo": ("sbuf", [128, 48], "float32"),
    "wl": ("sbuf", [128, 48], "bfloat16"), "ofs": ("sbuf", [128, 48], "uint16"),
}
for _b in range(8):
    SCRATCH["pb%d" % _b] = ("psum", [128, 512], "float32")

SEMAPHORES = (["cV", "cS", "cP", "cG", "go", "snd", "l_e", "l_w", "l_s", "l_n", "l_l", "l_a", "l_b", "aL", "aR", "aR0",
               "o_p0", "o_v0", "o_p1", "o_v1", "o_e"] + ["aL%d" % k for k in range(4)])

PARAMS = {
    'order': [[(3, 0), (0, 1), (2, 0), (1, 0), (3, 1), (2, 1), (0, 2), (1, 2), (3, 2)],
              [(2, 0), (1, 0), (0, 0), (3, 1), (3, 2), (2, 1), (0, 2), (1, 1), (2, 2)]],
    'small': {'ask': 'S', 'hh': 'S', 'f': 'V', 'm': 'S', 'm2': 'S', 'fs': 'S', 'uf': 'S', 'win': 'V', 'fu001': 'S', 'ufu032': 'V'},
    'g1': [0, 0, 48, 64, 0, 24, 0, 24, 32, 0, 0, 64, 24, 48, 0, 0, 0, 0],
    'g2': [16, 0, 16, 24, 24, 16, 16, 16, 16, 16, 0, 16, 16, 0, 48, 32, 48, 16],
    'eps': {'V': 0, 'S': 0.05, 'P': 0.05},
    'bonus': {'db': -2.1, 'x2': 0.2, 'sc16': 0.6, 'u122': 3.6, 'pc': 4.8, 'u112': 2.5, 'u111': 1.3, 'm2': 2.4, 'hh': -1.1, 'ab': 0.7,
              'j13': 0.4, 'st': -2.4, 'u101': 0.2, 'u011': -3.5, 'sc8': 0.7, 'x1': 0.3, 'u121': -0.7, 'u031': 0.2, 'as': 0.6, 'j00': 0.9,
              'u012': 0.4, 'j11': -0.9, 'u022': 4.4, 'u102': -0.2, 't3': 2.0, 'sc0': 4.1, 'j12': 3.4, 'mi': 0.8, 'hi': -0.1, 'u131': 0.4,
              'j03': -0.2, 'u100': -0.3, 'u001': 1.4, 'j10': 3.8, 'uf': -0.2, 'sl': 0.1, 'u010': 0.8, 'mm': -0.1, 'sc32': 8.9,
              'u130': -0.1, 'set': -3.9, 'fs': -0.4, 'u030': -0.7, 'lo': -0.1},
    'pc': [0, 3, 1, 2], 'chunks': [(8, 16), (0, 8), (16, 32), (32, 48)],
}
MODEL = {"cy": 0.83e-3 * 1.25, "pe": 0.42e-3 * 1.25, "G": 1.56, "SC": 3.8, "x": 0.10, "own": 0.06, "fix": 0.02,
         "db": 4.5, "rem": 2.5}
CACHE = {}


def build(g, core, T, topo, prm, md):
    ops = []
    last_w, readers = {}, {}
    cur = ["set"]
    cy, pe = md["cy"], md["pe"]
    V, SC, P = g.vector, g.scalar, g.tensor

    def add(eng, fn, rd, wr, cost, banks=(), sem=None, lat=0.0, name=""):
        n = len(ops)
        deps = {}
        for r in rd:
            if r in last_w: deps[last_w[r]] = True
        for r in wr:
            if r in last_w: deps.setdefault(last_w[r], False)
            for x in readers.get(r, []): deps.setdefault(x, False)
        for r in rd: readers.setdefault(r, []).append(n)
        for r in wr:
            last_w[r] = n
            readers[r] = []
        deps.pop(n, None)
        ops.append({"eng": eng, "fn": fn, "deps": deps, "cost": cost, "banks": tuple(banks), "sem": sem, "lat": lat, "name": name,
                    "unit": cur[0]})

    def cyc(n): return md["fix"] + max(64, n) * cy
    def bk(names): return sorted(set(int(r[1]) for r in names if r[0] == "@"))

    def ts(out, in0, s1, s2, o0, o1, rd, wr, n=64):
        if o1 is None: fn = lambda: [V.tensor_scalar(out, in0, s1, None, o0)]
        else: fn = lambda: [V.tensor_scalar(out, in0, s1, s2, o0, o1)]
        add("V", fn, rd, wr, cyc(n), bk(rd + wr), name=wr[0])

    def tt(out, a, b, op, rd, wr, n=64):
        add("V", lambda: [V.tensor_tensor(out, a, b, op)], rd, wr, cyc(n), bk(rd + wr), name=wr[0])

    def cp(out, a, rd, wr, n=64):
        add("V", lambda: [V.tensor_copy(out, a)], rd, wr, cyc(n), bk(rd + wr), name=wr[0])

    def ms(out, val, wr, n=64, rd=()):
        add("V", lambda: [V.memset(out, val)], list(rd), wr, cyc(n), name=wr[0])

    def scan(out, d0, d1, init, o0, o1, rd, wr, n):
        add("V", lambda: [V.tensor_tensor_scan(out, d0, d1, init, o0, o1)], rd, wr, cyc(n), name=wr[0])

    def act(out, a, f, bias, scale, rd, wr, n=64):
        add("S", lambda: [SC.activation(out, a, f, bias=bias, scale=scale)], rd, wr, cyc(n), bk(rd + wr), name=wr[0])

    def aff(e, out, a, scale, bias, rd, wr, relu=False):
        if e == "S": act(out, a, F.Relu if relu else F.Identity, bias, scale, rd, wr)
        elif relu: ts(out, a, bias, 0.0, A.add, A.max, rd, wr)
        elif scale == 1.0: ts(out, a, bias, None, A.add, None, rd, wr)
        else: ts(out, a, scale, bias, A.mult, A.add, rd, wr)

    def mm(groups, rd, wr, cols):
        def fn():
            res = []
            for out, terms in groups:
                for i, (l, r) in enumerate(terms):
                    ins = P.matmul(out, l, r, i == 0, i == len(terms) - 1)
                res.append(ins)
            return res
        add("P", fn, rd, wr, md["fix"] + cols * pe, bk(rd + wr), name=wr[0])

    def iota(out, pat, base, cm, wr, n, flt=True):
        if flt: fn = lambda: [g.iota(out, pat, base, cm, allow_small_or_imprecise_dtypes=True)]
        else: fn = lambda: [g.iota(out, pat, base, cm)]
        add("G", fn, [], wr, 0.15 + 2 * n * cy, name=wr[0])

    def dma(e, out, a, rd, wr, sem, lat):
        q = {"Y": g.sync, "S": g.scalar}[e]
        add(e, lambda: [q.dma_start(out, a)], rd, wr, 0.1, sem=(sem, 16), lat=lat, name=sem)

    def ps(b, r, rows=128): return T["pb%d" % b][0:rows, 64 * r:64 * r + 64]
    def pn(b, r): return "@%d.%d" % (b, r)

    rank = T.rank_of(core)
    N = len(T.cores)
    nxt, prv = T.cores[(rank + 1) % N], T.cores[(rank - 1) % N]

    def send(dst, src, land, sem, rd, tag):
        rid, pid = topo.addr(dst)[:2]
        mask = sum(1 << e for e in topo.engines(core, dst)[0::2])
        def fn():
            g.remote_dma(land, src, T.sem[sem], T.sem.snd, pid, rid, mask)
            return []
        add("G", fn, rd, ["sent" + tag], 0.4, name="send" + tag)
        add(None, None, ["sent" + tag], [tag], 0.0, sem=(sem, 8), lat=md["rem"], name=sem)

    dma("Y", T.eown[:], T.ends[:], [], ["eown"], "l_e", 2.0)
    dma("S", T.wts[:], T.wt[:], [], ["wts"], "l_w", 2.0)
    dma("S", T.slt[:], T.salt[:], [], ["slt"], "l_s", 2.2)
    dma("Y", T.win[:, DB0:DB0 + W // 2], T.db[:, 0:W // 2], [], ["dbA"], "l_a", 2.0 + md["db"])
    dma("S", T.nzs[:], T.nz[:], [], ["nzs"], "l_n", 3.0)
    dma("S", T.sli[0:8, :], T.sl[:], [], ["sli"], "l_l", 3.0)

    names = ["id", "idm1", "idm4", "idm256", "idk", "idmk", "idh", "idq", "idr", "bo", "bom", "lt", "bo15", "w64", "w256"]
    CB = {n: T.cb[:, 128 * i:128 * i + 128] for i, n in enumerate(names)}
    IDF, BOF, G8 = T.cf[:, 0:128], T.cf[:, 128:256], T.cf[0:8, 256:384]
    cn = ["gk", "q15", "h05", "h025", "h1", "g3", "bF", "p16", "hq"]
    CO = {n: T.col[:, i:i + 1] for i, n in enumerate(cn)}
    iota(T.pi[:, 0:1], [[0, 1]], 0, 1, ["pi"], 1, False)
    iota(T.gm[:], [[16, 8], [0, 16]], 0, 0, ["gm"], 128)
    iota(T.jm[:], [[1, 128]], 0, -1, ["jm"], 128)
    send(nxt, T.eown[:], T.lft0[:], "aL", ["eown"], "lft0")
    add("G", lambda: [g.sem_inc(T.sem.go, 1)], ["sentlft0"], ["go"], 0.02, sem=("go", 1), name="go")
    dma("Y", T.win[:, DB0 + W // 2:FS0], T.db[:, W // 2:W], ["go"], ["dbB"], "l_b", 0.0)
    add(None, None, ["dbB", "dbA"], ["dbT"], 0.0, lat=md["db"], name="dbT")
    send(prv, T.eown[:], T.rgt0[:], "aR", ["eown", "go"], "rgt0")
    iota(T.j34[:], [[1, 34]], 0, 0, ["j34"], 34)
    iota(T.fc[:], [[1, 64 * NSLOT]], FS0, 0, ["fc"], 64 * NSLOT)
    iota(T.jd[:], [[-16, 4], [1, 64]], 0, -1, ["jd"], 256)
    iota(T.dum0[:], [[0, 12], [16, 4]], 0, 1, ["dum0"], 48)
    ts(T.pi[:, 1:2], T.pi[:, 0:1], 4, None, A.arith_shift_right, None, ["pi"], ["gi"])
    ts(T.pi[:, 2:3], T.pi[:, 0:1], 15, None, A.bitwise_and, None, ["pi"], ["qi"])
    ts(CO["gk"], T.pi[:, 1:2], 16.0, None, A.mult, None, ["gi"], ["gk"])
    ts(BOF, T.gm[:], CO["gk"], None, A.is_equal, None, ["gm", "gk"], ["bof"], 128)
    for b in range(8):
        ts(T.cb[:, 13 * 128 + 16 * b:13 * 128 + 16 * b + 16], T.wts[:], T.cf[:, 128 + 16 * b:129 + 16 * b], 1.0 / 64, A.mult, A.mult,
           ["wts", "bof"], ["w64.%d" % b])
    W64 = ["w64.%d" % b for b in range(8)]
    act(CB["w256"], CB["w64"], F.Identity, 0.0, 0.25, W64, ["w256"], 128)
    for i, val in enumerate([-63.0 / 128, -255.0 / 512, -0.375]):
        ms(T.cst[0:1, 128 * i:128 * i + 128], val, ["cst%d" % i])
    ms(T.cst[0:1, 384:448], 1.0, ["one"])
    C0, C1, C2, ONE = T.cst[0:1, 0:128], T.cst[0:1, 128:256], T.cst[0:1, 256:384], T.cst[0:1, 384:448]
    for s in range(S):
        ts(T.s8[:, 256 * s:256 * s + 256], T.slt[:], float(211 * s - 2738 + W), 8.0, A.add, A.mult, ["slt"], ["s8.%d" % s], 256)
    ts(IDF, T.jm[:], 0.0, None, A.is_equal, None, ["jm"], ["idf"], 128)
    for n, val in (("id", 1.0), ("idm1", -1.0), ("idm4", -4.0), ("idm256", -256.0), ("idk", 1.0 / K), ("idmk", -1.0 / K)):
        act(CB[n], IDF, F.Identity, 0.0, val, ["idf"], [n], 128)
    ts(CO["q15"], T.pi[:, 2:3], 15.0, None, A.is_equal, None, ["qi"], ["q15"])
    for n, c, val in (("idh", "h05", 0.5), ("idq", "h025", 0.25), ("idr", "h1", 1.0)):
        ts(CO[c], T.pi[:, 2:3], 15.0, val, A.not_equal, A.mult, ["qi"], [c])
        act(CB[n], IDF, F.Identity, 0.0, CO[c], ["idf", c], [n], 128)
    act(T.z15[:, 0:128], IDF, F.Identity, 0.0, CO["q15"], ["idf", "q15"], ["z15a"], 128)
    ms(T.z15[:, 128:144], 0.0, ["z15b"])
    act(CB["bo"], BOF, F.Identity, 0.0, 1.0, ["bof"], ["bo"], 128)
    act(CB["bom"], BOF, F.Identity, 0.0, -1.0, ["bof"], ["bom"], 128)
    ts(T.jd2[:, 0:128], T.jm[:], 0.0, -1.0, A.is_gt, A.mult, ["jm"], ["lt0"], 128)
    tt(T.jd2[:, 128:256], T.jd2[:, 0:128], IDF, A.add, ["lt0", "idf"], ["lt1"], 256)
    tt(CB["lt"], T.jd2[:, 128:256], BOF, A.mult, ["lt1", "bof"], ["lt"], 256)
    ms(T.mall[:], K, ["mall"])
    ms(T.win[:, 0:DB0], 0.0, ["spare"])
    ms(T.d0x[:], 1.0, ["d0x"], 512)
    ms(T.d0x[:, 0::16], 0.0, ["d0x"], rd=["d0x"])
    ms(T.d0n[:], 0.0, ["d0n"], 512)
    ms(T.d0n[:, 0::16], 1024.0, ["d0n"], rd=["d0n"])
    ms(CB["bo15"], 0.0, ["bo15"])
    cp(T.cb[:, 12 * 128 + 15:13 * 128:16], T.cf[:, 128 + 15:256:16], ["bof", "bo15"], ["bo15"])
    ms(T.yy[:], 0.0, ["yy"], 144)
    cp(T.yy[:, 15:128:16], T.cf[:, 128 + 15:256:16], ["bof", "yy"], ["yy"])
    ts(CO["g3"], T.pi[:, 1:2], 3.0, 2.0, A.mult, A.add, ["gi"], ["g3"])
    ts(CO["p16"], T.pi[:, 0:1], 16.0, None, A.mult, None, ["pi"], ["p16"])
    ts(T.yb[:], T.j34[:], CO["g3"], None, A.is_equal, None, ["j34", "g3"], ["yb"])
    ts(G8, T.gm[0:8, :], T.col[0:8, 7:8], -1.0, A.is_equal, A.mult, ["gm", "p16"], ["g8"], 128)
    ts(CO["bF"], T.pi[:, 2:3], 15.0, -192.0, A.is_equal, A.mult, ["qi"], ["bF"])
    ts(CO["hq"], T.pi[:, 2:3], 15.0, 0.5, A.is_lt, A.mult, ["qi"], ["hq0"])
    ts(CO["hq"], CO["hq"], 0.5, None, A.add, None, ["hq0"], ["hq"])
    cp(T.slf[0:8, :], T.sli[0:8, :], ["sli"], ["slf"], 512)
    ts(T.dum[:], T.dum0[:], CO["gk"], None, A.subtract, None, ["dum0", "gk"], ["dum"])
    ts(T.jd[:], T.jd[:], CO["gk"], None, A.add, None, ["jd", "gk"], ["jd"], 256)
    ts(T.jd3[:], T.jd[:], 0.0, -0.5, A.is_ge, A.mult, ["jd"], ["jd3"], 256)
    ts(T.jd[:], T.jd[:], 2.0, 0.5, A.is_ge, A.mult, ["jd", "jd3"], ["jd"], 256)
    tt(T.jd[:], T.jd[:], T.jd3[:], A.add, ["jd", "jd3"], ["jd"], 512)
    DW = ["dw0", "dw1", "dw2", "dw3"]
    for R in range(4):
        act(T.dw[:, 256 * R:256 * R + 256], T.jd[:], F.Identity, 1.0, 1.0, ["jd"], [DW[R]], 256)
    ms(T.dw[:, 0::64], 2097152.0, DW, rd=DW)

    def sm(x): return prm["small"].get(x + cur[0], prm["small"][x])

    def pick(out, win, off, nv, rd, wr):
        res = []
        for e, a, b in (("V", 0, nv), ("S", nv, 64)):
            if a == b: continue
            o, src = out(16 * a, 16 * b), win.indirect(off(a, b))
            if e == "V": fn = lambda o=o, src=src: [V.tensor_copy(o, src)]
            else: fn = lambda o=o, src=src: [SC.activation(o, src, F.Copy)]
            add(e, fn, rd, [wr + e], (0.06 if e == "V" else 0.08) + 16 * (b - a) * md["G"] * cy, name=wr + e)
            res.append(wr + e)
        return res

    def side(m, k): return ((4, 0), (5, 0), (4, 4), (6, 0))[k] if m == 0 else (4 + k, 0)

    def unit(m, k, s, v, vn):
        c = slice(64 * k, 64 * k + 64)
        bA = k
        bB, r0 = side(m, k)
        cur[0] = "u%d%d%d" % (m, k, s)
        heavy = (k + m) % 4 != s
        n = lambda x: x + str(k)
        nzv = T.nzs[:, (m * 3 + s) * 256 + k:(m * 3 + s + 1) * 256:4]
        mm([(ps(bA, 0), [(CB["w64"], v), (C0, ONE)]), (ps(bA, 1), [(CB["w256"], v), (C1, ONE)])],
           [vn, "w256", "cst0", "cst1", "one"] + W64, [pn(bA, 0), pn(bA, 1)], 256)
        aff(sm("uf"), T.uf[:, c], ps(bA, 0), 1.0, MG, [pn(bA, 0)], [n("uf")])
        if heavy or m == 0:
            ts(T.kb[:, c], ps(bA, 1), MG, MG, A.add, A.subtract, [pn(bA, 1)], [n("kb")])
        act(ps(bA, 2), T.uf[:, c], F.Square, 148.0 - MG, 1.0, [n("uf")], [pn(bA, 2)])
        tt(T.wi[:, c], ps(bA, 2), T.s8[:, 256 * s + k:256 * s + 256:4], A.add, [pn(bA, 2), "s8.%d" % s], [n("wi")])
        ts(T.pl[:, c], T.wi[:, c], 3, W - 1, A.arith_shift_right, A.bitwise_and, [n("wi")], [n("pl")])
        if heavy: cp(T.of1[:, c], T.pl[:, c], [n("pl")], [n("of1")])
        ts(T.plf[:, c], T.pl[:, c], float(DB0), None, A.add, None, [n("pl")], [n("plf")])
        if heavy or m == 0:
            mm([(ps(bA, 3), [(CB["w64"], v), (C0, ONE), (CB["idm4"], T.kb[:, c])])], [vn, "cst0", "one", "idm4", n("kb")] + W64, [pn(bA, 3)], 192)
            aff(sm("ask"), T.ask[:, c], ps(bA, 3), 1.0, 192.0, [pn(bA, 3)], [n("ask")])
        mm([(ps(bB, r0), [(CB["id"], v), (CB["id"], nzv)])], [vn, "id", "nzs"], [pn(bB, r0)], 128)
        aff(sm("hh"), T.hh[:, c], ps(bB, r0), 1.0 / 256, 192.0 - 255.0 / 512, [pn(bB, r0)], [n("hh")])
        mm([(ps(bB, r0 + 1), [(CB["id"], v), (CB["id"], nzv), (CB["idm256"], T.hh[:, c])])], [vn, "id", "nzs", "idm256", n("hh")],
           [pn(bB, r0 + 1)], 192)
        if heavy:
            t = prm["order"][m].index((k, s)) + 9 * m
            f, fn_ = T.win[:, FS0 + 64 * t:FS0 + 64 * t + 64], "slot%d" % t
        else:
            f, fn_ = T.fsk[:, c], n("fsk")
        aff(sm("f"), f, ps(bB, r0 + 1), 1.0, 49152.0, [pn(bB, r0 + 1)], [fn_])
        vo, von = T.vb[:, 256 * s + 64 * k:256 * s + 64 * k + 64], "vb%d%d" % (s, k)
        x0 = 1024 * k
        if heavy:
            p1 = pick(lambda a, b: T.x1[:, x0 + a:x0 + b], T.win[:, DB0:FS0], lambda a, b: T.of1[:, 64 * k + a:64 * k + b], prm["g1"][t],
                      [n("of1"), "dbA", "dbB", "dbT"], n("x1"))
            mm([(ps(bA, 0), [(CB["idm1"], T.ask[:, c])] + [(T.z15[:, 15 - p:143 - p], T.x1[:, x0 + p:x0 + 1024:16]) for p in range(16)])],
               p1 + ["idm1", n("ask"), "z15a", "z15b"], [pn(bA, 0)], 64 * 17)
            ts(T.mis[:, c], ps(bA, 0), -192.0, K, A.not_equal, A.mult, [pn(bA, 0)], [n("mis")])
            mis, misn = T.mis[:, c], n("mis")
            mm([(ps(bA, 1), [(IDF, T.plf[:, c]), (CB["id"], mis)])], ["idf", "id", n("plf"), misn], [pn(bA, 1)], 320)
            tt(T.t3[:, c], ps(bA, 1), T.fc[:, 64 * t:64 * t + 64], A.min, [pn(bA, 1), "fc"], [n("t3")])
            cp(T.of2[:, c], T.t3[:, c], [n("t3")], [n("of2")])
            p2 = pick(lambda a, b: T.x2[:, x0 + a:x0 + b], T.win[:, 0:FS0 + 64 * t + 64], lambda a, b: T.of2[:, 64 * k + a:64 * k + b],
                      prm["g2"][t], [n("of2"), "dbA", "dbB", "dbT", "spare"] + ["slot%d" % j for j in range(t + 1)], n("x2"))
            xs = T.x2[:, x0:x0 + 1024]
            scan(T.hi[:, x0:x0 + 1024], T.d0x[:], xs, 0.0, A.mult, A.max, p2 + ["d0x"], [n("hi")], 512)
            scan(T.lo[:, x0:x0 + 1024], T.d0n[:], xs, 0.0, A.add, A.min, p2 + ["d0n"], [n("lo")], 512)
            mm([(ps(bA, 2), [(CB["idh"], v), (C2, ONE), (CB["idq"], T.hi[:, x0 + 15:x0 + 1024:16]), (CB["idq"], T.lo[:, x0 + 15:x0 + 1024:16])])],
               [vn, "idh", "idq", "cst2", "one", n("hi"), n("lo")], [pn(bA, 2)], 256)
        else:
            mis, misn = T.mall[:], "mall"
            mm([(ps(bA, 2), [(CB["idh"], v), (C2, ONE), (CB["idh"], f)])], [vn, "idh", "cst2", "one", fn_], [pn(bA, 2)], 192)
        ts(vo, ps(bA, 2), MG, MG, A.add, A.subtract, [pn(bA, 2)], [von])
        m0 = 768 * m + 192 * k + 64 * s
        mm([(ps(bB, r0 + 2), [(IDF, T.plf[:, c]), (CB["lt"], mis)])], ["idf", "lt", n("plf"), misn], [pn(bB, r0 + 2)], 320)
        aff(sm("m"), T.mm[:, m0:m0 + 64], ps(bB, r0 + 2), 1.0, -K, [pn(bB, r0 + 2)], ["mm%d%d%d" % (m, k, s)], True)
        if m == 0:
            mm([(ps(bB, r0 + 3), [(CB["id"], T.ask[:, c]), (CB["lt"], mis)])], ["id", "lt", n("ask"), misn], [pn(bB, r0 + 3)], 128)
            aff(sm("m2"), T.m2[:, c], ps(bB, r0 + 3), 1.0, -K, [pn(bB, r0 + 3)], [n("m2")], True)
            mm([(ps(bB, r0 + 3), [(CB["idr"], f), (CB["bo15"], T.m2[:, c])])], ["idr", "bo15", fn_, n("m2")], [pn(bB, r0 + 3)], 128)
            aff(sm("fs"), T.fsh[:, 256 * s + k:256 * s + 256:4], ps(bB, r0 + 3), 1.0, CO["bF"], [pn(bB, r0 + 3), "bF"], ["fsh%d%d" % (s, k)])
        return vo, von

    def judge(m, k, v, vn, e, en_, t, tn):
        c = slice(64 * k, 64 * k + 64)
        bA = k
        bB, r0 = side(m, k)
        cur[0] = "j%d%d" % (m, k)
        n = lambda x: x + str(k)
        mm([(ps(bA, 0), [(CB["idm1"], t), (CB["id"], v)]), (ps(bA, 3), [(CB["idk"], e), (CB["idmk"], v)])],
           ["id", "idm1", "idk", "idmk", vn, tn, en_], [pn(bA, 0), pn(bA, 3)], 256)
        act(T.da[:, c], ps(bA, 0), F.Abs, 0.0, 1.0, [pn(bA, 0)], [n("da")])
        mm([(ps(bA, 1), [(G8, T.slf[0:8, 256 * m + k:256 * m + 256:4]), (CB["bom"], T.dbb[:, c]), (CB["bo"], T.da[:, c])])],
           ["g8", "slf", "bo", "bom", n("da"), n("dbb")], [pn(bA, 1)], 384)
        ts(T.nac[:, c], ps(bA, 1), 0.0, K, A.is_gt, A.mult, [pn(bA, 1)], [n("nac")])
        if m == 0:
            for s in range(S):
                m0 = 192 * k + 64 * s
                mm([(T["pb%d" % s][:, 256 + k:512:4], [(BOF, T.mm[:, m0:m0 + 64]), (CB["id"], T.nac[:, c])])],
                   ["bof", "id", "mm0%d%d" % (k, s), n("nac")], ["@%d.r%d%d" % (s, s, k)], 320)
        tt(T.td[:, c], ps(bA, 3), T.nac[:, c], A.mult, [pn(bA, 3), n("nac")], [n("td")])
        if m == 0:
            tt(T.enew[:, c], T.td[:, c], v, A.add, [n("td"), vn], [n("enew")], 128)
            send(nxt, T.enew[:, c], T.lft1[:, c], "aL%d" % k, [n("enew")], "lft1%d" % k)
        else:
            tt(T.eout[:, k::4], T.td[:, c], v, A.add, [n("td"), vn], [n("eout")], 128)
        st = T["st%d" % m]
        m0 = 768 * m + 192 * k
        mm([(ps(bB, r0 + 2, 32), [(T.yb[:, 2 - s:34 - s], T.mm[:, m0 + 64 * s:m0 + 64 * s + 64]) for s in range(S)])],
           ["yb"] + ["mm%d%d%d" % (m, k, s) for s in range(S)], [pn(bB, r0 + 2)], 768)
        ts(st[0:32, k::4], ps(bB, r0 + 2, 32), -float(DB0), -1.0, A.add, A.max, [pn(bB, r0 + 2)], ["st%d%d" % (m, k)])
        act(T.sv[:, 256 * m + k:256 * m + 256:4], T.nac[:, c], F.Identity, 1.0, -1.0 / K, [n("nac")], ["sv%d%d" % (m, k)])

    for m in range(RU):
        state = {}
        for k in range(4):
            c = slice(64 * k, 64 * k + 64)
            if m == 0: state[k] = [T.lft0[:, k::4], "lft0", T.eown[:, k::4], "eown", T.rgt0[:, k::4], "rgt0"]
            else: state[k] = [T.lft1[:, c], "lft1%d" % k, T.enew[:, c], "enew%d" % k, T.rgt1[:, c], "rgt1"]
        done = {k: 0 for k in range(4)}
        for k, s in prm["order"][m] + [(k, 2) for k in range(4)]:
            while done[k] <= s:
                if done[k] == 2:
                    e, en_, t, tn = state[k][2:]
                    mm([(ps(k, 3), [(CB["id"], e), (CB["idm1"], t)])], ["id", "idm1", en_, tn], [pn(k, 3)], 128)
                    act(T.dbb[:, 64 * k:64 * k + 64], ps(k, 3), F.Abs, 0.0, 1.0, [pn(k, 3)], ["dbb%d" % k])
                state[k][0], state[k][1] = unit(m, k, done[k], state[k][0], state[k][1])
                done[k] += 1
        if m == 0:
            cur[0] = "pc"
            pcol = T.pb7[:, 256:304]
            for j, k in enumerate(prm["pc"]):
                def part(j=j, k=k):
                    for i in range(4):
                        q = 4 * i + k
                        ins = P.matmul(pcol, T.yy[:, 15 - q:143 - q], T.mm[:, 192 * k + i:192 * k + 192:4], j + i == 0, j + i == 6)
                    return [ins]
                add("P", part, ["yy"] + ["mm0%d%d" % (k, s) for s in range(S)], ["@7.pc"], md["fix"] + 1024 * pe, [7], name="@7.pc")
            tt(T.pc[:], pcol, T.dum[:], A.subtract, ["@7.pc", "dum"], ["pc0"])
            act(T.pc[:], T.pc[:], F.Relu, 0.0, 1.0, ["pc0"], ["pc"])
            act(T.nb[:], pcol, F.Identity, 1.0, -8.0, ["@7.pc"], ["nb"])
            act(T.nb[:, 3::4], T.pb7[:, 259:304:4], F.Identity, CO["hq"], -8.0, ["@7.pc", "hq", "nb"], ["nb"])
        for k in range(4):
            judge(m, k, *state[k])
        if m == 0: send(prv, T.enew[:], T.rgt1[:], "aR0", ["enew%d" % k for k in range(4)], "rgt1")
        cur[0] = "out"
        dma("Y", T.yp[:, 768 * m:768 * m + 768], T["st%d" % m][0:24, :], ["st%d%d" % (m, k) for k in range(4)], ["yp%d" % m], "o_p%d" % m, 2.0)
        if m == 1: dma("Y", T.ye[:], T.eout[:], ["eout%d" % k for k in range(4)], ["ye"], "o_e", 2.0)
        dma("Y" if m == 0 else "S", T.yv[:, 256 * m:256 * m + 256], T.sv[0::16, 256 * m:256 * m + 256],
            ["sv%d%d" % (m, k) for k in range(4)], ["yv%d" % m], "o_v%d" % m, 2.0)
        if m == 0:
            cur[0] = "ab"
            for s in range(S):
                for r in range(16):
                    R = r // 4
                    act(T.ab[:, 1024 * s + 64 * r:1024 * s + 64 * r + 64], T["pb%d" % s][:, 256 + 64 * R:256 + 64 * R + 64], F.Abs,
                        T.nb[:, 16 * s + r:16 * s + r + 1], 8.0, ["nb"] + ["@%d.r%d%d" % (s, s, k) for k in range(4)], ["ab%d.%d" % (s, r)])
            for a, b in prm["chunks"]:
                tag = str(a)
                cur[0] = "sc" + tag
                for a1 in range(a, b, 16):
                    b1 = min(b, a1 + 16)
                    scan(T.sc[:, 64 * a1:64 * b1], T.dw[:, 0:64 * (b1 - a1)], T.ab[:, 64 * a1:64 * b1], 1.0, A.mult, A.min,
                         DW + ["ab%d.%d" % (r // 16, r % 16) for r in range(a1, b1)], ["sc%d" % a1], 32 * (b1 - a1))
                last, scs = T.sc[:, 64 * a + 63:64 * b:64], ["sc%d" % a1 for a1 in range(a, b, 16)]
                if sm("win") == "V":
                    ts(T.wn[:, a:b], last, 0.5, None, A.is_equal, None, scs, ["wn" + tag])
                    tt(T.wp[:, a:b], T.wn[:, a:b], T.pc[:, a:b], A.mult, ["wn" + tag, "pc"], ["wp" + tag])
                    tt(T.wo[:, a:b], T.wp[:, a:b], T.dum[:, a:b], A.add, ["wp" + tag, "dum"], ["wo" + tag])
                    cp(T.ofs[:, a:b], T.wo[:, a:b], ["wo" + tag], ["ofs" + tag])
                else:
                    z1, z2 = T.pb7[:, 320 + a:320 + b], T.pb7[:, 384 + a:384 + b]
                    act(T.wl[:, a:b], last, F.Abs, -2 * K, 4 * K, scs, ["wn" + tag])
                    mm([(z1, [(IDF, T.pc[:, a:b]), (CB["idm1"], T.wl[:, a:b])])], ["idf", "idm1", "pc", "wn" + tag], ["@7.y" + tag], 320)
                    act(T.wp[:, a:b], z1, F.Relu, 0.0, 1.0, ["@7.y" + tag], ["wp" + tag])
                    mm([(z2, [(IDF, T.dum[:, a:b]), (IDF, T.wp[:, a:b])])], ["idf", "dum", "wp" + tag], ["@7.z" + tag], 512)
                    cp(T.ofs[:, a:b], z2, ["@7.z" + tag], ["ofs" + tag])
                for s, R in [(s, R) for s in range(S) for R in (3, 2, 1, 0) if a <= 16 * s + 4 * R < b]:
                    dst = T.win[:, 0:FS0].indirect(T.ofs[:, 16 * s + 4 * R:16 * s + 4 * R + 4])
                    src = T.fsh[:, 256 * s + 64 * R:256 * s + 64 * R + 64]
                    add("V", lambda dst=dst, src=src: [V.tensor_copy(dst, src)], ["ofs" + tag] + ["fsh%d%d" % (s, k) for k in range(4)],
                        ["dbA", "dbB", "dbT", "spare"], 0.06 + 64 * md["SC"] * cy, name="scat")
    return ops


def gap(a, b, raw, md):
    if a["eng"] is None or b["eng"] is None: return a["lat"]
    if a["sem"] is not None: return a["lat"] + md["x"]
    if a["eng"] == b["eng"]: return md["own"]
    return md["x"]


def schedule(ops, md, prm):
    n = len(ops)
    succ = [[] for _ in range(n)]
    for i, o in enumerate(ops):
        for d, raw in o["deps"].items(): succ[d].append((i, raw))
    prio = [0.0] * n
    for i in range(n - 1, -1, -1):
        prio[i] = ops[i]["cost"] + max([gap(ops[i], ops[j], raw, md) + prio[j] for j, raw in succ[i]] + [ops[i]["lat"]])
    eps = prm["eps"]
    for i in range(n): prio[i] += prm["bonus"].get(ops[i]["unit"], 0.0) + prm["bonus"].get(ops[i]["name"][:2], 0.0)
    left = [len(o["deps"]) for o in ops]
    ready_t = [0.0] * n
    ready = [i for i in range(n) if left[i] == 0]
    free, bank, fin = {}, {}, [0.0] * n
    order, extra = [], {}
    while ready:
        est = {}
        for i in ready:
            o = ops[i]
            t = max(ready_t[i], free.get(o["eng"], 0.0)) if o["eng"] else ready_t[i]
            for b in o["banks"]:
                if b in bank and ops[bank[b]]["eng"] != o["eng"]: t = max(t, fin[bank[b]] + md["x"])
            est[i] = t
        t0 = min(est.values())
        i = max((j for j in ready if est[j] <= t0 + eps.get(ops[j]["eng"], 0.0)), key=lambda j: (prio[j], -j))
        o = ops[i]
        fin[i] = est[i] + o["cost"]
        if o["eng"]: free[o["eng"]] = fin[i]
        extra[i] = [bank[b] for b in o["banks"] if b in bank and ops[bank[b]]["eng"] != o["eng"]]
        for b in o["banks"]: bank[b] = i
        order.append(i)
        ready.remove(i)
        for j, raw in succ[i]:
            ready_t[j] = max(ready_t[j], fin[i] + gap(o, ops[j], raw, md))
            left[j] -= 1
            if left[j] == 0: ready.append(j)
    return order, extra


def rank_program(g, core, T, topo):
    if T.rank_of(core) is None:
        return
    ops = build(g, core, T, topo, PARAMS, MODEL)
    if "plan" not in CACHE: CACHE["plan"] = schedule(ops, MODEL, PARAMS)
    order, extra = CACHE["plan"]
    Q = {"V": g.vector, "S": g.scalar, "P": g.tensor, "G": g, "Y": g.sync}
    count = {}
    known = {e: {} for e in Q}
    mark = {}
    for i in order:
        o = ops[i]
        e = o["eng"]
        if e is None:
            if o["sem"]:
                count[o["sem"][0]] = o["sem"][1]
                mark[i] = [(o["sem"][0], o["sem"][1], {})]
            else:
                mark[i] = [x for d in o["deps"] for x in mark[d]]
            continue
        waits = {}
        for d in list(o["deps"]) + extra[i]:
            for sname, val, kn in mark[d]:
                if known[e].get(sname, 0) < val and waits.get(sname, (0,))[0] < val: waits[sname] = (val, kn)
        for sname in sorted(waits, key=lambda x: -len(waits[x][1])):
            val, kn = waits[sname]
            if known[e].get(sname, 0) >= val: continue
            Q[e].wait_ge(T.sem[sname], val)
            known[e][sname] = val
            for a, b in kn.items():
                if known[e].get(a, 0) < b: known[e][a] = b
        res = o["fn"]()
        if o["sem"]:
            if o["sem"][1] == 16: res[0].then_inc(T.sem[o["sem"][0]], 16)
            count[o["sem"][0]] = o["sem"][1]
            mark[i] = [(o["sem"][0], o["sem"][1], dict(known[e]))]
        elif res:
            for ins in res:
                ins.then_inc(T.sem["c" + e], 1)
                count["c" + e] = count.get("c" + e, 0) + 1
            mark[i] = [("c" + e, count["c" + e], dict(known[e]))]
        else:
            count["snd"] = count.get("snd", 0) + 8
            mark[i] = []
    for sname in sorted(count):
        g.wait_ge(T.sem[sname], count[sname])
